import numpy as np
import ml_dtypes


def mxq(x, axis, fmt="e4m3"):
    dtype, down = {"e4m3": (ml_dtypes.float8_e4m3fn, 7), "e5m2": (ml_dtypes.float8_e5m2, 14)}[fmt]
    v = np.moveaxis(np.asarray(x, np.float32).astype(ml_dtypes.bfloat16).astype(np.float64), axis, -1)
    blocks = v.reshape(v.shape[:-1] + (-1, 32))
    amax = np.abs(blocks).max(-1, keepdims=True)
    byte = np.maximum(np.where(amax > 0, np.frexp(amax)[1] - 1 + 127, 0) - down, 1)
    scale = np.exp2(byte - 127.0)
    codes = (blocks / scale).astype(np.float32).astype(dtype).astype(np.float64)
    return np.moveaxis((codes * scale).reshape(v.shape), -1, axis)


WIDE = False


def mx_kscale(k):
    if not WIDE:
        return np.ones(k)
    levels = np.array([10, -10, 5, -5, 0])
    if k % 512:
        return np.exp2(np.random.permutation(np.resize(levels, k // 32))).repeat(32)
    a = np.empty((k // 512, 16))
    for p in range(k // 512):
        a[p, :8] = np.random.permutation(np.resize(levels, 8))
        for g in range(8):
            far = levels[np.abs(levels - a[p, g]) >= 10]
            a[p, g + 8] = far[np.random.randint(len(far))]
    return np.exp2(a.ravel()).repeat(32)


def f64(x):
    return np.asarray(x).astype(np.float64)


def striped(idx):
    return np.tile(idx.reshape(-1, 16).T, (8, 1)).astype(np.uint16)


def unstriped(offs):
    return offs[:16].T.reshape(-1).astype(np.int64)


E2M1 = np.array([0.0, 0.5, 1.0, 1.5, 2.0, 3.0, 4.0, 6.0, -0.0, -0.5, -1.0, -1.5, -2.0, -3.0, -4.0, -6.0])


def pack_weight(w, fmt):
    k, n = w.shape
    w = f64(np.asarray(w, np.float32).astype(ml_dtypes.bfloat16)).reshape(k // 32, 32, n)
    amax = np.abs(w).max(1)
    if fmt == "e4m3":
        byte = np.frexp(amax)[1] - 1 + 127 - 7
    else:
        mant, ex = np.frexp(amax / 6.0)
        byte = np.where(mant > 0.5, ex, ex - 1) + 127
    byte = np.clip(np.where(amax > 0, byte, 1), 1, 254)
    scaled = (w * np.exp2(127.0 - byte)[:, None, :]).reshape(k, n).astype(np.float32)
    by_word = np.ascontiguousarray(scaled.reshape(k // 512, 128, 4, n).transpose(0, 1, 3, 2))
    if fmt == "e4m3":
        words = by_word.astype(ml_dtypes.float8_e4m3fn).view(np.uint8)
    else:
        c = by_word.astype(ml_dtypes.float4_e2m1fn).view(np.uint8) & 0xF
        words = (c[..., 0::2] | (c[..., 1::2] << 4)).reshape(k // 512, 128, 2 * n)
    return np.ascontiguousarray(words), np.ascontiguousarray(byte.astype(np.uint8).reshape(k // 512, 16, n))


def unpack_weight(words, scales, fmt):
    g, _, n = scales.shape
    words = np.ascontiguousarray(words).reshape(g, 128, n, -1)
    if fmt == "e4m3":
        vals = words.view(ml_dtypes.float8_e4m3fn).astype(np.float64)
    else:
        nib = np.empty((g, 128, n, 4), np.uint8)
        nib[..., 0::2] = words & 0xF
        nib[..., 1::2] = words >> 4
        vals = E2M1[nib]
    vals = vals * np.repeat(np.exp2(scales.astype(np.float64) - 127.0), 8, axis=1)[..., None]
    return vals.transpose(0, 1, 3, 2).reshape(g * 512, n)


def gelu(v):
    return 0.5 * v * (1.0 + np.tanh(np.sqrt(2.0 / np.pi) * (v + 0.044715 * v**3)))


def bf(x):
    return np.asarray(x, np.float32).astype(ml_dtypes.bfloat16)


def planes(Y):
    n, m = Y.shape
    b = f64(bf(Y)).reshape(n // 32, 32, m)
    amax = np.abs(b).max(1)
    byte = np.clip(np.where(amax > 0, np.frexp(amax)[1] - 1 + 127 - 7, 1), 1, 254)
    codes = (b * np.exp2(127.0 - byte)[:, None, :]).reshape(n, m).astype(np.float32).astype(ml_dtypes.float8_e4m3fn).view(np.uint8)
    words = codes.reshape(n // 512, 128, 4, m).transpose(0, 1, 3, 2)
    return np.ascontiguousarray(words), np.ascontiguousarray(byte.astype(np.uint8).reshape(n // 512, 16, m))


K, K2, T, T2, S, P, H, N = 1536, 512, 4096, 2048, 1024, 512, 1024, 512

def setup_inputs():
    n = np.random.standard_normal
    s = mx_kscale(K)[:, None]
    s2 = mx_kscale(K2)[:, None]
    u = mx_kscale(H)[:, None]
    size = np.exp(0.8 * n(N))
    d = {}
    d["tab_words"], d["tab_scales"] = pack_weight(n((K, T)) * s, "e4m3")
    d["tab2_words"], d["tab2_scales"] = pack_weight(n((K2, T2)) * s2, "e4m3")
    d["offs"] = striped(np.random.permutation(T)[:S])
    d["offs2"] = striped(np.random.permutation(T2)[:P])
    d["pos1"] = striped(np.random.permutation(S)[:P])
    d["w1"] = (1.5 * n((K, H)) / K ** 0.5 / s).astype(np.float32)
    d["gain"] = (0.6 * np.exp(0.3 * n(H)) * u[:, 0]).astype(np.float32)
    d["w2_words"], d["w2_scales"] = pack_weight(n((K2, H)) / K2 ** 0.5 / s2 * u.T, "e2m1")
    d["blank"] = (0.8 * n(H) * u[:, 0]).astype(np.float32)
    d["wgs"] = np.exp(0.3 * n((128, P))).astype(np.float32)
    d["w4"] = (n((H, N)) / H ** 0.5 / u * size[None, :]).astype(np.float32)
    d["lot"] = (n((N, S)) * size[:, None]).astype(np.float32)
    return d

def reference(tab_words, tab_scales, tab2_words, tab2_scales, offs, offs2, pos1, w1, gain, w2_words, w2_scales, blank, wgs, w4, lot):
    v = unpack_weight(tab_words, tab_scales, "e4m3")[:, unstriped(offs)]
    v2 = unpack_weight(tab2_words, tab2_scales, "e4m3")[:, unstriped(offs2)]
    w2 = unpack_weight(w2_words, w2_scales, "e2m1")
    f = mxq(f64(w1), 0, "e4m3").T @ v
    a = f64(gain)[:, None] * (f + np.tanh(f))
    b = (w2.T @ v2) + f64(blank)[:, None]
    placed = np.zeros((H, S))
    placed[:, unstriped(pos1)] = np.tile(f64(wgs), (H // 128, 1)) * b
    z = a + placed
    y = (mxq(f64(w4), 0, "e4m3").T @ mxq(z, 0, "e4m3")) + f64(lot)
    words, scales = planes(y)
    return y, words, scales

@@ -1,0 +1,268 @@
+from contextlib import ExitStack
+
+import concourse.mybir as mybir
+from concourse.masks import make_identity
+
+K, K2, T, T2, S, PL, H, N = 1536, 512, 4096, 2048, 1024, 512, 1024, 512
+FLOPS = 2 * (K * H * S + K2 * H * PL + H * N * S)
+
+F32 = mybir.dt.float32
+BF16 = mybir.dt.bfloat16
+I32 = mybir.dt.int32
+U32 = mybir.dt.uint32
+U16 = mybir.dt.uint16
+U8 = mybir.dt.uint8
+FP8X4 = mybir.dt.float8_e4m3fn_x4
+FP4X4 = mybir.dt.float4_e2m1fn_x4
+ACT = mybir.ActivationFunctionType
+ALU = mybir.AluOpType
+
+P = 128
+PACK = 4
+KP = P * PACK
+HALF = 512
+Z_ON_SCALAR = {(0, 0): 0, (1, 0): 0, (0, 1): 512, (1, 1): 160}
+Y_ON_SCALAR = {0: 512, 1: 160}
+
+
+def tile_list_cork_taint_features_kernel(
+    tc, tab_words, tab_scales, tab2_words, tab2_scales, offs, offs2, pos1, w1, gain,
+    w2_words, w2_scales, blank, wgs, w4, lot, out_0, out_1, out_2,
+):
+    nc = tc.nc
+
+    def weave(dst, src, on_scalar):
+        n = src.shape[2]
+        for engine_copy, c0, c1 in ((nc.scalar.copy, 0, on_scalar), (nc.vector.tensor_copy, on_scalar, n)):
+            if c1 > c0:
+                engine_copy(
+                    out=dst[:, c0:c1, :].rearrange("p (c i) t -> p c t i", i=4),
+                    in_=src[:, :, c0:c1].rearrange("p t (c i) -> p c t i", i=4),
+                )
+
+    def quantize(codes, scales, woven):
+        nc.vector.quantize_mx(out=codes.bitcast(FP8X4), scales=scales, in_=woven)
+
+    with ExitStack() as ctx:
+        lists = ctx.enter_context(tc.tile_pool(name="lists", bufs=1))
+        keep = ctx.enter_context(tc.tile_pool(name="keep", bufs=1))
+        early = ctx.enter_context(tc.tile_pool(name="early", bufs=1))
+        big = ctx.enter_context(tc.tile_pool(name="big", bufs=3))
+        raw = ctx.enter_context(tc.tile_pool(name="raw", bufs=5))
+        stage = ctx.enter_context(tc.tile_pool(name="stage", bufs=2))
+        bpool = ctx.enter_context(tc.tile_pool(name="bpool", bufs=4))
+        ps_f = ctx.enter_context(tc.psum_pool(name="ps_f", bufs=2))
+        ps_u = ctx.enter_context(tc.psum_pool(name="ps_u", bufs=4))
+        ps_o = ctx.enter_context(tc.psum_pool(name="ps_o", bufs=2))
+
+        t2_scale = early.tile([P, T2], U8, offset=8192, align_bytes=64)
+        w2_scale = early.tile([P, H], U8, offset=14336, align_bytes=64)
+        t1_scale = keep.tile([P, T], U8, align_bytes=64)
+        nc.vector.memset(w2_scale[:].bitcast(I32), 0)
+        nc.vector.memset(t2_scale[:].bitcast(I32), 0)
+        nc.vector.memset(t1_scale[:].bitcast(I32), 0)
+        order = [(g, t) for t in range(PACK) for g in range(2)]
+        pages = {}
+        for g, t in order[:4]:
+            pages[g, t] = keep.tile([P, S], F32, name=f"page{g}{t}")
+            nc.vector.memset(pages[g, t][:], 0.0)
+
+        for q in range(4):
+            nc.sync.dma_start(w2_scale[32 * q : 32 * q + 4, :].bitcast(I32), w2_scales[0, 4 * q : 4 * q + 4, :].bitcast(I32))
+        for q in range(4):
+            nc.sync.dma_start(t2_scale[32 * q : 32 * q + 4, :].bitcast(I32), tab2_scales[0, 4 * q : 4 * q + 4, :].bitcast(I32))
+        idx2 = lists.tile([P, PL // 16], U16)
+        nc.sync.dma_start(idx2[:], offs2)
+        w2_code = early.tile([P, 2 * H], U8, offset=12288, align_bytes=64)
+        nc.sync.dma_start(w2_code[:].bitcast(I32), w2_words[0].bitcast(I32))
+        t2_code = early.tile([P, T2], I32, offset=0, align_bytes=64)
+        nc.sync.dma_start(t2_code[:], tab2_words[0].rearrange("p n t -> p (n t)").bitcast(I32))
+        seats = lists.tile([P, PL // 16], U16)
+        nc.sync.dma_start(seats[:], pos1)
+        idx = lists.tile([P, S // 16], U16)
+        nc.sync.dma_start(idx[:], offs)
+        blank_rows = blank.rearrange("(g p t) -> p g t", g=2, t=PACK)
+        blank_early = keep.tile([P, 2, PACK - 1], F32)
+        nc.sync.dma_start(blank_early[:], blank_rows[:, :, : PACK - 1])
+        gain_sb = keep.tile([P, 2, PACK], F32)
+        nc.sync.dma_start(gain_sb[:], gain.rearrange("(g p t) -> p g t", g=2, t=PACK))
+        wgs_sb = keep.tile([P, PACK, PL], F32)
+        for q in range(4):
+            nc.sync.dma_start(wgs_sb[32 * q : 32 * q + 32, :, :], wgs.rearrange("(p t) j -> p t j", t=PACK))
+        ident = keep.tile([P, P], F32)
+        make_identity(nc, ident[:])
+
+        w1_raw = {}
+        for g in range(2):
+            for a in range(3):
+                w1_raw[a, g] = raw.tile([P, PACK, HALF], F32, name="raw")
+                nc.sync.dma_start(
+                    w1_raw[a, g][:],
+                    w1[a * KP : (a + 1) * KP, g * KP : (g + 1) * KP].rearrange("(p i) c -> p i c", i=PACK),
+                )
+        w4_raw = {}
+        for g in range(2):
+            w4_raw[g] = raw.tile([P, PACK, N], F32, name="raw")
+            nc.sync.dma_start(w4_raw[g][:], w4[g * KP : (g + 1) * KP, :].rearrange("(p i) c -> p i c", i=PACK))
+        for q in range(4):
+            nc.sync.dma_start(t1_scale[32 * q : 32 * q + 12, :].bitcast(I32), tab_scales[:, 4 * q : 4 * q + 4, :].bitcast(I32))
+        t1_code = []
+        for a in range(3):
+            t1_code.append(big.tile([P, T], I32, name="big", align_bytes=64))
+            nc.sync.dma_start(t1_code[a][:], tab_words[a].rearrange("p n t -> p (n t)").bitcast(I32))
+        blank_late = keep.tile([P, 2, 1], F32)
+        with nc.allow_non_contiguous_dma(reason="one value a row"):
+            nc.sync.dma_start(blank_late[:], blank_rows[:, :, PACK - 1 :])
+        lot_rows = lot.rearrange("(p t) j -> p t j", t=PACK)
+        y_sb = []
+        for h in range(2):
+            y_sb.append(raw.tile([P, PACK, HALF], F32, name="raw"))
+            nc.sync.dma_start(y_sb[h][:], lot_rows[:, :, h * HALF : (h + 1) * HALF])
+
+        w2_dealt = keep.tile([P, 2, PACK, P, 2], U8, align_bytes=64)
+        w2_scale_dealt = keep.tile([P, 2, PACK, P], U8, align_bytes=64)
+        w2_view = w2_code[:].rearrange("p (g m t b) -> p g t m b", g=2, t=PACK, b=2)
+        nc.vector.tensor_copy(w2_dealt[:, 0], w2_view[:, 0])
+        v2_code = keep.tile([P, PL], U32, align_bytes=64)
+        v2_scale = keep.tile([P, PL], U8, align_bytes=64)
+        nc.vector.tensor_copy(v2_code[:], t2_code[:].bitcast(U32).indirect(idx2[:]))
+        nc.vector.tensor_copy(w2_scale_dealt[:], w2_scale[:].rearrange("p (g m t) -> p g t m", g=2, t=PACK))
+        nc.vector.tensor_copy(v2_scale[:], t2_scale[:].indirect(idx2[:]))
+        nc.vector.tensor_copy(w2_dealt[:, 1], w2_view[:, 1])
+
+        for n, (g, t) in enumerate(order[4:]):
+            pages[g, t] = early.tile([P, S], F32, name=f"page{g}{t}", offset=4096 * n, align_bytes=64)
+            nc.gpsimd.memset(pages[g, t][:], 0.0)
+
+        v_scale = keep.tile([P, S], U8, align_bytes=64)
+        nc.vector.tensor_copy(v_scale[:], t1_scale[:].indirect(idx[:]))
+        v_code = [keep.tile([P, S], U32, name=f"v_code{a}", align_bytes=64) for a in range(3)]
+        for a in range(3):
+            for h in range(2):
+                nc.vector.tensor_copy(
+                    v_code[a][:, h * HALF : (h + 1) * HALF],
+                    t1_code[a][:].bitcast(U32).indirect(idx[:, h * HALF // 16 : (h + 1) * HALF // 16]),
+                )
+
+        for g, t in order:
+            bias = blank_early[:, g, t : t + 1] if t < PACK - 1 else blank_late[:, g, :]
+            acc_b = ps_o.tile([P, PL], F32, name="acc_o")
+            nc.tensor.matmul_mx(
+                out=acc_b[:],
+                lhsT=w2_dealt[:, g, t].rearrange("p m b -> p (m b)").bitcast(FP4X4),
+                lhsT_scale=w2_scale_dealt[:, g, t, :],
+                rhs=v2_code[:].bitcast(FP8X4),
+                rhs_scale=v2_scale[:],
+                start=True,
+                stop=True,
+            )
+            b_sb = bpool.tile([P, PL], F32)
+            nc.scalar.activation(b_sb[:], acc_b[:], ACT.Identity, bias=bias)
+            nc.vector.tensor_tensor(pages[g, t][:].indirect(seats[:]), b_sb[:], wgs_sb[:, t, :], ALU.mult)
+
+        w1_code, w1_scale, w4_code, w4_scale = {}, {}, {}, {}
+        for g in range(2):
+            for a in range(3):
+                woven_w = stage.tile([P, HALF, PACK], BF16, name="woven_w", align_bytes=64)
+                weave(woven_w, w1_raw[a, g], HALF)
+                w1_code[a, g] = keep.tile([P, HALF], U32, name=f"w1_code{a}{g}", align_bytes=64)
+                w1_scale[a, g] = keep.tile([P, HALF], U8, name=f"w1_scale{a}{g}", align_bytes=64)
+                quantize(w1_code[a, g][:], w1_scale[a, g][:], woven_w[:].rearrange("p c i -> p (c i)"))
+        for g in range(2):
+            woven_w = stage.tile([P, N, PACK], BF16, name="woven_w", align_bytes=64)
+            nc.scalar.copy(
+                out=woven_w[:].rearrange("p (t m) i -> p m i t", t=PACK),
+                in_=w4_raw[g][:].rearrange("p i (m t) -> p m i t", t=PACK),
+            )
+            w4_code[g] = keep.tile([P, N], U32, name=f"w4_code{g}", align_bytes=64)
+            w4_scale[g] = keep.tile([P, N], U8, name=f"w4_scale{g}", align_bytes=64)
+            quantize(w4_code[g][:], w4_scale[g][:], woven_w[:].rearrange("p c i -> p (c i)"))
+
+        z_code, z_scale = {}, {}
+
+        def first_stage(g, h):
+            terms = big.tile([P, 4, 2, KP], F32, name="big", align_bytes=64)
+            for jt in range(4):
+                cols = slice(h * HALF + jt * P, h * HALF + (jt + 1) * P)
+                acc_f = ps_f.tile([P, KP], F32)
+                for a in range(3):
+                    nc.tensor.matmul_mx(
+                        out=acc_f[:],
+                        lhsT=v_code[a][:, cols].bitcast(FP8X4),
+                        lhsT_scale=v_scale[4 * a : P, cols],
+                        rhs=w1_code[a, g][:].bitcast(FP8X4),
+                        rhs_scale=w1_scale[a, g][:],
+                        start=(a == 0),
+                        stop=(a == 2),
+                    )
+                dealt = acc_f[:].rearrange("j (p t) -> j t p", t=PACK)
+                nc.scalar.activation(terms[:, jt, 0, :].rearrange("j (t p) -> j t p", t=PACK), dealt, ACT.Tanh)
+                nc.scalar.copy(terms[:, jt, 1, :].rearrange("j (t p) -> j t p", t=PACK), dealt)
+            return terms
+
+        def make_z(g, h, terms):
+            z_rows = stage.tile([P, PACK, HALF], BF16, name="z_rows")
+            for t in range(PACK):
+                acc_u = ps_u.tile([P, HALF], F32)
+                for jt in range(4):
+                    for term in range(2):
+                        nc.tensor.matmul(
+                            acc_u[:, jt * P : (jt + 1) * P],
+                            terms[:, jt, term, t * P : (t + 1) * P],
+                            ident[:],
+                            start=(term == 0),
+                            stop=(term == 1),
+                            is_transpose=True,
+                        )
+                nc.vector.scalar_tensor_tensor(
+                    out=z_rows[:, t, :],
+                    in0=acc_u[:],
+                    scalar=gain_sb[:, g, t : t + 1],
+                    in1=pages[g, t][:, h * HALF : (h + 1) * HALF],
+                    op0=ALU.mult,
+                    op1=ALU.add,
+                )
+            woven = stage.tile([P, HALF, PACK], BF16, name="woven", align_bytes=64)
+            weave(woven, z_rows, Z_ON_SCALAR[g, h])
+            z_code[g, h] = keep.tile([P, HALF], U32, name=f"z_code{g}{h}", align_bytes=64)
+            z_scale[g, h] = keep.tile([P, HALF], U8, name=f"z_scale{g}{h}", align_bytes=64)
+            quantize(z_code[g, h][:], z_scale[g, h][:], woven[:].rearrange("p c i -> p (c i)"))
+
+        out_rows = out_0.rearrange("(p t) j -> p t j", t=PACK)
+        out_words = out_1[0].rearrange("p m t -> p (m t)").bitcast(I32)
+
+        def last_stage(h):
+            cols = slice(h * HALF, (h + 1) * HALF)
+            for t in range(PACK):
+                acc_y = ps_o.tile([P, HALF], F32, name="acc_o")
+                for g in range(2):
+                    nc.tensor.matmul_mx(
+                        out=acc_y[:],
+                        lhsT=w4_code[g][:, t * P : (t + 1) * P].bitcast(FP8X4),
+                        lhsT_scale=w4_scale[g][:, t * P : (t + 1) * P],
+                        rhs=z_code[g, h][:].bitcast(FP8X4),
+                        rhs_scale=z_scale[g, h][:],
+                        start=(g == 0),
+                        stop=(g == 1),
+                    )
+                nc.vector.tensor_tensor(y_sb[h][:, t, :], acc_y[:], y_sb[h][:, t, :], ALU.add)
+                nc.sync.dma_start(out_rows[:, t, cols], y_sb[h][:, t, :])
+            woven = stage.tile([P, HALF, PACK], BF16, name="woven", align_bytes=64)
+            weave(woven, y_sb[h], Y_ON_SCALAR[h])
+            y_code = keep.tile([P, HALF], U32, name=f"y_code{h}", align_bytes=64)
+            y_scale = keep.tile([P, HALF], U8, name=f"y_scale{h}", align_bytes=64)
+            quantize(y_code[:], y_scale[:], woven[:].rearrange("p c i -> p (c i)"))
+            nc.sync.dma_start(out_words[:, cols], y_code[:].bitcast(I32))
+            for q in range(4):
+                nc.sync.dma_start(
+                    out_2[0, 4 * q : 4 * q + 4, cols].bitcast(I32), y_scale[32 * q : 32 * q + 4, :].bitcast(I32)
+                )
+
+        groups = [(g, h) for h in range(2) for g in range(2)]
+        terms = first_stage(*groups[0])
+        for n, (g, h) in enumerate(groups):
+            following = first_stage(*groups[n + 1]) if n + 1 < len(groups) else None
+            make_z(g, h, terms)
+            if g == 1:
+                last_stage(h)
+            terms = following

@@ -1,7 +1,6 @@
 from contextlib import ExitStack
 
 import concourse.mybir as mybir
-from concourse.masks import make_identity
 
 K, K2, T, T2, S, PL, H, N = 1536, 512, 4096, 2048, 1024, 512, 1024, 512
 FLOPS = 2 * (K * H * S + K2 * H * PL + H * N * S)
@@ -21,8 +20,8 @@ P = 128
 PACK = 4
 KP = P * PACK
 HALF = 512
-Z_ON_SCALAR = {(0, 0): 0, (1, 0): 0, (0, 1): 512, (1, 1): 160}
-Y_ON_SCALAR = {0: 512, 1: 160}
+Z_ON_SCALAR = {(0, 0): 0, (1, 0): 512, (0, 1): 512, (1, 1): 176}
+Y_ON_SCALAR = {0: 512, 1: 176}
 
 
 def tile_list_cork_taint_features_kernel(
@@ -49,48 +48,43 @@ def tile_list_cork_taint_features_kernel(
         early = ctx.enter_context(tc.tile_pool(name="early", bufs=1))
         big = ctx.enter_context(tc.tile_pool(name="big", bufs=3))
         raw = ctx.enter_context(tc.tile_pool(name="raw", bufs=5))
-        stage = ctx.enter_context(tc.tile_pool(name="stage", bufs=2))
-        bpool = ctx.enter_context(tc.tile_pool(name="bpool", bufs=4))
-        ps_f = ctx.enter_context(tc.psum_pool(name="ps_f", bufs=2))
-        ps_u = ctx.enter_context(tc.psum_pool(name="ps_u", bufs=4))
-        ps_o = ctx.enter_context(tc.psum_pool(name="ps_o", bufs=2))
+        rows = ctx.enter_context(tc.tile_pool(name="rows", bufs=4))
+        stage = ctx.enter_context(tc.tile_pool(name="stage", bufs=8))
+        psum = ctx.enter_context(tc.psum_pool(name="psum", bufs=8))
 
         t2_scale = early.tile([P, T2], U8, offset=8192, align_bytes=64)
         w2_scale = early.tile([P, H], U8, offset=14336, align_bytes=64)
         t1_scale = keep.tile([P, T], U8, align_bytes=64)
-        nc.vector.memset(w2_scale[:].bitcast(I32), 0)
+        nc.gpsimd.memset(w2_scale[:].bitcast(I32), 0)
+        blank_rows = blank.rearrange("(g p t) -> p g t", g=2, t=PACK)
+        blank_early = keep.tile([P, 2, PACK - 1], F32)
+        nc.gpsimd.dma_start(blank_early[:], blank_rows[:, :, : PACK - 1])
         nc.vector.memset(t2_scale[:].bitcast(I32), 0)
-        nc.vector.memset(t1_scale[:].bitcast(I32), 0)
         order = [(g, t) for t in range(PACK) for g in range(2)]
         pages = {}
-        for g, t in order[:4]:
+        for n, (g, t) in enumerate(order[:4]):
             pages[g, t] = keep.tile([P, S], F32, name=f"page{g}{t}")
-            nc.vector.memset(pages[g, t][:], 0.0)
+            (nc.vector if n < 2 else nc.gpsimd).memset(pages[g, t][:].bitcast(I32), 0)
+        nc.gpsimd.memset(t1_scale[:].bitcast(I32), 0)
 
-        for q in range(4):
-            nc.sync.dma_start(w2_scale[32 * q : 32 * q + 4, :].bitcast(I32), w2_scales[0, 4 * q : 4 * q + 4, :].bitcast(I32))
-        for q in range(4):
-            nc.sync.dma_start(t2_scale[32 * q : 32 * q + 4, :].bitcast(I32), tab2_scales[0, 4 * q : 4 * q + 4, :].bitcast(I32))
+        def load_scale_rows(plane, rows, q):
+            nc.sync.dma_start(plane[32 * q : 32 * q + 4, :].bitcast(I32), rows[4 * q : 4 * q + 4, :].bitcast(I32))
+
         idx2 = lists.tile([P, PL // 16], U16)
         nc.sync.dma_start(idx2[:], offs2)
+        seats = lists.tile([P, PL // 16], U16)
+        nc.sync.dma_start(seats[:], pos1)
+        for q in range(4):
+            load_scale_rows(w2_scale, w2_scales[0], q)
         w2_code = early.tile([P, 2 * H], U8, offset=12288, align_bytes=64)
         nc.sync.dma_start(w2_code[:].bitcast(I32), w2_words[0].bitcast(I32))
         t2_code = early.tile([P, T2], I32, offset=0, align_bytes=64)
         nc.sync.dma_start(t2_code[:], tab2_words[0].rearrange("p n t -> p (n t)").bitcast(I32))
-        seats = lists.tile([P, PL // 16], U16)
-        nc.sync.dma_start(seats[:], pos1)
-        idx = lists.tile([P, S // 16], U16)
-        nc.sync.dma_start(idx[:], offs)
-        blank_rows = blank.rearrange("(g p t) -> p g t", g=2, t=PACK)
-        blank_early = keep.tile([P, 2, PACK - 1], F32)
-        nc.sync.dma_start(blank_early[:], blank_rows[:, :, : PACK - 1])
-        gain_sb = keep.tile([P, 2, PACK], F32)
-        nc.sync.dma_start(gain_sb[:], gain.rearrange("(g p t) -> p g t", g=2, t=PACK))
+        for q in range(4):
+            load_scale_rows(t2_scale, tab2_scales[0], q)
         wgs_sb = keep.tile([P, PACK, PL], F32)
         for q in range(4):
             nc.sync.dma_start(wgs_sb[32 * q : 32 * q + 32, :, :], wgs.rearrange("(p t) j -> p t j", t=PACK))
-        ident = keep.tile([P, P], F32)
-        make_identity(nc, ident[:])
 
         w1_raw = {}
         for g in range(2):
@@ -104,6 +98,10 @@ def tile_list_cork_taint_features_kernel(
         for g in range(2):
             w4_raw[g] = raw.tile([P, PACK, N], F32, name="raw")
             nc.sync.dma_start(w4_raw[g][:], w4[g * KP : (g + 1) * KP, :].rearrange("(p i) c -> p i c", i=PACK))
+        idx = lists.tile([P, S // 16], U16)
+        nc.sync.dma_start(idx[:], offs)
+        gain_sb = keep.tile([P, 2, PACK], F32)
+        nc.sync.dma_start(gain_sb[:], gain.rearrange("(g p t) -> p g t", g=2, t=PACK))
         for q in range(4):
             nc.sync.dma_start(t1_scale[32 * q : 32 * q + 12, :].bitcast(I32), tab_scales[:, 4 * q : 4 * q + 4, :].bitcast(I32))
         t1_code = []
@@ -119,109 +117,108 @@ def tile_list_cork_taint_features_kernel(
             y_sb.append(raw.tile([P, PACK, HALF], F32, name="raw"))
             nc.sync.dma_start(y_sb[h][:], lot_rows[:, :, h * HALF : (h + 1) * HALF])
 
-        w2_dealt = keep.tile([P, 2, PACK, P, 2], U8, align_bytes=64)
+        w2_dealt = keep.tile([P, 2, PACK, P], U16, align_bytes=64)
         w2_scale_dealt = keep.tile([P, 2, PACK, P], U8, align_bytes=64)
-        w2_view = w2_code[:].rearrange("p (g m t b) -> p g t m b", g=2, t=PACK, b=2)
-        nc.vector.tensor_copy(w2_dealt[:, 0], w2_view[:, 0])
+        w2_view = w2_code[:].bitcast(U16).rearrange("p (g m t) -> p g t m", g=2, t=PACK)
+        nc.vector.tensor_copy(w2_dealt[:], w2_view)
+        nc.vector.tensor_copy(w2_scale_dealt[:], w2_scale[:].rearrange("p (g m t) -> p g t m", g=2, t=PACK))
         v2_code = keep.tile([P, PL], U32, align_bytes=64)
         v2_scale = keep.tile([P, PL], U8, align_bytes=64)
-        nc.vector.tensor_copy(v2_code[:], t2_code[:].bitcast(U32).indirect(idx2[:]))
-        nc.vector.tensor_copy(w2_scale_dealt[:], w2_scale[:].rearrange("p (g m t) -> p g t m", g=2, t=PACK))
-        nc.vector.tensor_copy(v2_scale[:], t2_scale[:].indirect(idx2[:]))
-        nc.vector.tensor_copy(w2_dealt[:, 1], w2_view[:, 1])
-
+        list_halves = [(0, PL // 2), (PL // 2, PL)]
+        for j0, j1 in list_halves:
+            nc.vector.tensor_copy(v2_code[:, j0:j1], t2_code[:].bitcast(U32).indirect(idx2[:, j0 // 16 : j1 // 16]))
+            nc.vector.tensor_copy(v2_scale[:, j0:j1], t2_scale[:].indirect(idx2[:, j0 // 16 : j1 // 16]))
         for n, (g, t) in enumerate(order[4:]):
             pages[g, t] = early.tile([P, S], F32, name=f"page{g}{t}", offset=4096 * n, align_bytes=64)
-            nc.gpsimd.memset(pages[g, t][:], 0.0)
+            nc.gpsimd.memset(pages[g, t][:].bitcast(I32), 0)
 
         v_scale = keep.tile([P, S], U8, align_bytes=64)
         nc.vector.tensor_copy(v_scale[:], t1_scale[:].indirect(idx[:]))
         v_code = [keep.tile([P, S], U32, name=f"v_code{a}", align_bytes=64) for a in range(3)]
-        for a in range(3):
-            for h in range(2):
-                nc.vector.tensor_copy(
-                    v_code[a][:, h * HALF : (h + 1) * HALF],
-                    t1_code[a][:].bitcast(U32).indirect(idx[:, h * HALF // 16 : (h + 1) * HALF // 16]),
-                )
+        for a in range(2):
+            nc.vector.tensor_copy(v_code[a][:], t1_code[a][:].bitcast(U32).indirect(idx[:]))
+        for h in range(2):
+            nc.vector.tensor_copy(
+                v_code[2][:, h * HALF : (h + 1) * HALF],
+                t1_code[2][:].bitcast(U32).indirect(idx[:, h * HALF // 16 : (h + 1) * HALF // 16]),
+            )
 
         for g, t in order:
+            if g == 0:
+                b_pair = rows.tile([P, 2, PL], F32, name="rows")
             bias = blank_early[:, g, t : t + 1] if t < PACK - 1 else blank_late[:, g, :]
-            acc_b = ps_o.tile([P, PL], F32, name="acc_o")
-            nc.tensor.matmul_mx(
-                out=acc_b[:],
-                lhsT=w2_dealt[:, g, t].rearrange("p m b -> p (m b)").bitcast(FP4X4),
-                lhsT_scale=w2_scale_dealt[:, g, t, :],
-                rhs=v2_code[:].bitcast(FP8X4),
-                rhs_scale=v2_scale[:],
-                start=True,
-                stop=True,
-            )
-            b_sb = bpool.tile([P, PL], F32)
-            nc.scalar.activation(b_sb[:], acc_b[:], ACT.Identity, bias=bias)
-            nc.vector.tensor_tensor(pages[g, t][:].indirect(seats[:]), b_sb[:], wgs_sb[:, t, :], ALU.mult)
+            for j0, j1 in list_halves if (g, t) == order[0] else [(0, PL)]:
+                acc_b = psum.tile([P, PL], F32, name="acc")
+                nc.tensor.matmul_mx(
+                    out=acc_b[:, j0:j1],
+                    lhsT=w2_dealt[:, g, t, :].bitcast(FP4X4),
+                    lhsT_scale=w2_scale_dealt[:, g, t, :],
+                    rhs=v2_code[:, j0:j1].bitcast(FP8X4),
+                    rhs_scale=v2_scale[:, j0:j1],
+                    start=True,
+                    stop=True,
+                )
+                nc.scalar.activation(b_pair[:, g, j0:j1], acc_b[:, j0:j1], ACT.Identity, bias=bias)
+                nc.vector.tensor_tensor(
+                    pages[g, t][:].indirect(seats[:, j0 // 16 : j1 // 16]),
+                    b_pair[:, g, j0:j1],
+                    wgs_sb[:, t, j0:j1],
+                    ALU.mult,
+                )
+
+        def quantize_weight(raw_rows, dealt, name):
+            woven = stage.tile([P, HALF, PACK], BF16, name="woven", align_bytes=64)
+            if dealt:
+                nc.scalar.copy(
+                    out=woven[:].rearrange("p (t m) i -> p m i t", t=PACK),
+                    in_=raw_rows[:].rearrange("p i (m t) -> p m i t", t=PACK),
+                )
+            else:
+                weave(woven, raw_rows, HALF)
+            code = keep.tile([P, HALF], U32, name=name + "_code", align_bytes=64)
+            scale = keep.tile([P, HALF], U8, name=name + "_scale", align_bytes=64)
+            quantize(code[:], scale[:], woven[:].rearrange("p c i -> p (c i)"))
+            return code, scale
 
         w1_code, w1_scale, w4_code, w4_scale = {}, {}, {}, {}
         for g in range(2):
             for a in range(3):
-                woven_w = stage.tile([P, HALF, PACK], BF16, name="woven_w", align_bytes=64)
-                weave(woven_w, w1_raw[a, g], HALF)
-                w1_code[a, g] = keep.tile([P, HALF], U32, name=f"w1_code{a}{g}", align_bytes=64)
-                w1_scale[a, g] = keep.tile([P, HALF], U8, name=f"w1_scale{a}{g}", align_bytes=64)
-                quantize(w1_code[a, g][:], w1_scale[a, g][:], woven_w[:].rearrange("p c i -> p (c i)"))
+                w1_code[a, g], w1_scale[a, g] = quantize_weight(w1_raw[a, g], True, f"w1_{a}{g}")
         for g in range(2):
-            woven_w = stage.tile([P, N, PACK], BF16, name="woven_w", align_bytes=64)
-            nc.scalar.copy(
-                out=woven_w[:].rearrange("p (t m) i -> p m i t", t=PACK),
-                in_=w4_raw[g][:].rearrange("p i (m t) -> p m i t", t=PACK),
-            )
-            w4_code[g] = keep.tile([P, N], U32, name=f"w4_code{g}", align_bytes=64)
-            w4_scale[g] = keep.tile([P, N], U8, name=f"w4_scale{g}", align_bytes=64)
-            quantize(w4_code[g][:], w4_scale[g][:], woven_w[:].rearrange("p c i -> p (c i)"))
+            w4_code[g], w4_scale[g] = quantize_weight(w4_raw[g], True, f"w4_{g}")
 
         z_code, z_scale = {}, {}
 
-        def first_stage(g, h):
-            terms = big.tile([P, 4, 2, KP], F32, name="big", align_bytes=64)
-            for jt in range(4):
-                cols = slice(h * HALF + jt * P, h * HALF + (jt + 1) * P)
-                acc_f = ps_f.tile([P, KP], F32)
+        def make_z(g, h):
+            cols = slice(h * HALF, (h + 1) * HALF)
+            rest = big.tile([P, PACK, HALF], F32, name="big", align_bytes=64)
+            z_rows = rows.tile([P, PACK, HALF], BF16, name="rows")
+            for t in range(PACK):
+                acc_f = psum.tile([P, HALF], F32, name="acc")
                 for a in range(3):
                     nc.tensor.matmul_mx(
                         out=acc_f[:],
-                        lhsT=v_code[a][:, cols].bitcast(FP8X4),
-                        lhsT_scale=v_scale[4 * a : P, cols],
-                        rhs=w1_code[a, g][:].bitcast(FP8X4),
-                        rhs_scale=w1_scale[a, g][:],
+                        lhsT=w1_code[a, g][:, t * P : (t + 1) * P].bitcast(FP8X4),
+                        lhsT_scale=w1_scale[a, g][:, t * P : (t + 1) * P],
+                        rhs=v_code[a][:, cols].bitcast(FP8X4),
+                        rhs_scale=v_scale[4 * a : P, cols],
                         start=(a == 0),
                         stop=(a == 2),
                     )
-                dealt = acc_f[:].rearrange("j (p t) -> j t p", t=PACK)
-                nc.scalar.activation(terms[:, jt, 0, :].rearrange("j (t p) -> j t p", t=PACK), dealt, ACT.Tanh)
-                nc.scalar.copy(terms[:, jt, 1, :].rearrange("j (t p) -> j t p", t=PACK), dealt)
-            return terms
-
-        def make_z(g, h, terms):
-            z_rows = stage.tile([P, PACK, HALF], BF16, name="z_rows")
-            for t in range(PACK):
-                acc_u = ps_u.tile([P, HALF], F32)
-                for jt in range(4):
-                    for term in range(2):
-                        nc.tensor.matmul(
-                            acc_u[:, jt * P : (jt + 1) * P],
-                            terms[:, jt, term, t * P : (t + 1) * P],
-                            ident[:],
-                            start=(term == 0),
-                            stop=(term == 1),
-                            is_transpose=True,
-                        )
+                nc.scalar.activation(rest[:, t, :], acc_f[:], ACT.Tanh)
+                nc.scalar.activation(rest[:, t, :], rest[:, t, :], ACT.Copy, scale=gain_sb[:, g, t : t + 1])
+                nc.gpsimd.tensor_tensor(rest[:, t, :], rest[:, t, :], pages[g, t][:, cols], ALU.add)
                 nc.vector.scalar_tensor_tensor(
                     out=z_rows[:, t, :],
-                    in0=acc_u[:],
+                    in0=acc_f[:],
                     scalar=gain_sb[:, g, t : t + 1],
-                    in1=pages[g, t][:, h * HALF : (h + 1) * HALF],
+                    in1=rest[:, t, :],
                     op0=ALU.mult,
                     op1=ALU.add,
                 )
+            finish_z(g, h, z_rows)
+
+        def finish_z(g, h, z_rows):
             woven = stage.tile([P, HALF, PACK], BF16, name="woven", align_bytes=64)
             weave(woven, z_rows, Z_ON_SCALAR[g, h])
             z_code[g, h] = keep.tile([P, HALF], U32, name=f"z_code{g}{h}", align_bytes=64)
@@ -234,7 +231,7 @@ def tile_list_cork_taint_features_kernel(
         def last_stage(h):
             cols = slice(h * HALF, (h + 1) * HALF)
             for t in range(PACK):
-                acc_y = ps_o.tile([P, HALF], F32, name="acc_o")
+                acc_y = psum.tile([P, HALF], F32, name="acc")
                 for g in range(2):
                     nc.tensor.matmul_mx(
                         out=acc_y[:],
@@ -258,11 +255,9 @@ def tile_list_cork_taint_features_kernel(
                     out_2[0, 4 * q : 4 * q + 4, cols].bitcast(I32), y_scale[32 * q : 32 * q + 4, :].bitcast(I32)
                 )
 
-        groups = [(g, h) for h in range(2) for g in range(2)]
-        terms = first_stage(*groups[0])
-        for n, (g, h) in enumerate(groups):
-            following = first_stage(*groups[n + 1]) if n + 1 < len(groups) else None
-            make_z(g, h, terms)
-            if g == 1:
-                last_stage(h)
-            terms = following
+        make_z(0, 0)
+        make_z(1, 0)
+        make_z(0, 1)
+        last_stage(0)
+        make_z(1, 1)
+        last_stage(1)

@@ -1,9 +1,10 @@
 from contextlib import ExitStack
 
 import concourse.mybir as mybir
+from concourse.masks import make_identity
 
-K, K2, T, T2, S, PL, H, N = 1536, 512, 4096, 2048, 1024, 512, 1024, 512
-FLOPS = 2 * (K * H * S + K2 * H * PL + H * N * S)
+K, K2, T, T2, S, SOAKED, H, N = 1536, 512, 4096, 2048, 1024, 512, 1024, 512
+FLOPS = 2 * (K * H * S + K2 * H * SOAKED + H * N * S)
 
 F32 = mybir.dt.float32
 BF16 = mybir.dt.bfloat16
@@ -18,10 +19,12 @@ ALU = mybir.AluOpType
 
 P = 128
 PACK = 4
-KP = P * PACK
-HALF = 512
-Z_ON_SCALAR = {(0, 0): 0, (1, 0): 512, (0, 1): 512, (1, 1): 176}
-Y_ON_SCALAR = {0: 512, 1: 176}
+PASS = P * PACK
+BANK = 512
+PER_COL = 16
+PAGE_BYTES = 4 * S
+EARLY_T = 2
+LAST_WEAVE_ON_SCALAR = 176
 
 
 def tile_list_cork_taint_features_kernel(
@@ -30,17 +33,17 @@ def tile_list_cork_taint_features_kernel(
 ):
     nc = tc.nc
 
-    def weave(dst, src, on_scalar):
-        n = src.shape[2]
-        for engine_copy, c0, c1 in ((nc.scalar.copy, 0, on_scalar), (nc.vector.tensor_copy, on_scalar, n)):
-            if c1 > c0:
-                engine_copy(
-                    out=dst[:, c0:c1, :].rearrange("p (c i) t -> p c t i", i=4),
-                    in_=src[:, :, c0:c1].rearrange("p t (c i) -> p c t i", i=4),
-                )
+    def entries(offsets, j0, j1):
+        return offsets[:, j0 // PER_COL : j1 // PER_COL]
 
-    def quantize(codes, scales, woven):
-        nc.vector.quantize_mx(out=codes.bitcast(FP8X4), scales=scales, in_=woven)
+    def weave(woven, rows, on_scalar):
+        shares = ((nc.scalar.copy, 0, on_scalar), (nc.vector.tensor_copy, on_scalar, BANK))
+        for engine_copy, j0, j1 in shares:
+            if j1 > j0:
+                engine_copy(
+                    out=woven[:, j0:j1, :].rearrange("p (c i) t -> p c t i", i=4),
+                    in_=rows[:, :, j0:j1].rearrange("p t (c i) -> p c t i", i=4),
+                )
 
     with ExitStack() as ctx:
         lists = ctx.enter_context(tc.tile_pool(name="lists", bufs=1))
@@ -52,212 +55,258 @@ def tile_list_cork_taint_features_kernel(
         stage = ctx.enter_context(tc.tile_pool(name="stage", bufs=8))
         psum = ctx.enter_context(tc.psum_pool(name="psum", bufs=8))
 
-        t2_scale = early.tile([P, T2], U8, offset=8192, align_bytes=64)
-        w2_scale = early.tile([P, H], U8, offset=14336, align_bytes=64)
+        def bank():
+            return psum.tile([P, BANK], F32, name="bank")
+
+        def woven_tile():
+            return stage.tile([P, BANK, PACK], BF16, name="woven", align_bytes=64)
+
+        def quantize(woven, name):
+            code = keep.tile([P, BANK], U32, name=name + "_code", align_bytes=64)
+            scale = keep.tile([P, BANK], U8, name=name + "_scale", align_bytes=64)
+            nc.vector.quantize_mx(
+                out=code[:].bitcast(FP8X4), scales=scale[:], in_=woven[:].rearrange("p j t -> p (j t)")
+            )
+            return code, scale
+
+        t2_scale = early.tile([P, T2], U8, offset=2 * PAGE_BYTES, align_bytes=64)
+        w2_scale = early.tile([P, H], U8, offset=3 * PAGE_BYTES + 2 * H, align_bytes=64)
         t1_scale = keep.tile([P, T], U8, align_bytes=64)
         nc.gpsimd.memset(w2_scale[:].bitcast(I32), 0)
         blank_rows = blank.rearrange("(g p t) -> p g t", g=2, t=PACK)
-        blank_early = keep.tile([P, 2, PACK - 1], F32)
-        nc.gpsimd.dma_start(blank_early[:], blank_rows[:, :, : PACK - 1])
+        blank_g0 = keep.tile([P, PACK], F32)
+        nc.gpsimd.dma_start(blank_g0[:], blank_rows[:, 0, :])
+        blank_g1_early = keep.tile([P, EARLY_T], F32)
+        nc.gpsimd.dma_start(blank_g1_early[:], blank_rows[:, 1, :EARLY_T])
         nc.vector.memset(t2_scale[:].bitcast(I32), 0)
-        order = [(g, t) for t in range(PACK) for g in range(2)]
         pages = {}
-        for n, (g, t) in enumerate(order[:4]):
-            pages[g, t] = keep.tile([P, S], F32, name=f"page{g}{t}")
-            (nc.vector if n < 2 else nc.gpsimd).memset(pages[g, t][:].bitcast(I32), 0)
+        for t in range(PACK):
+            pages[0, t] = keep.tile([P, S], F32, name=f"page0{t}")
+            (nc.vector if t < 2 else nc.gpsimd).memset(pages[0, t][:].bitcast(I32), 0)
         nc.gpsimd.memset(t1_scale[:].bitcast(I32), 0)
+        ident = keep.tile([P, P], F32)
+        make_identity(nc, ident[:])
 
-        def load_scale_rows(plane, rows, q):
-            nc.sync.dma_start(plane[32 * q : 32 * q + 4, :].bitcast(I32), rows[4 * q : 4 * q + 4, :].bitcast(I32))
+        def load_scale_rows(plane, scale_rows):
+            passes = scale_rows.shape[0]
+            for u in range(4):
+                nc.sync.dma_start(
+                    plane[32 * u : 32 * u + 4 * passes, :].bitcast(I32),
+                    scale_rows[:, 4 * u : 4 * u + 4, :].bitcast(I32),
+                )
 
-        idx2 = lists.tile([P, PL // 16], U16)
+        def load_rows(source):
+            piece = raw.tile([P, PACK, BANK], F32, name="raw")
+            nc.sync.dma_start(piece[:], source.rearrange("(p i) c -> p i c", i=PACK))
+            return piece
+
+        idx2 = lists.tile([P, SOAKED // PER_COL], U16)
         nc.sync.dma_start(idx2[:], offs2)
-        seats = lists.tile([P, PL // 16], U16)
+        seats = lists.tile([P, SOAKED // PER_COL], U16)
         nc.sync.dma_start(seats[:], pos1)
-        for q in range(4):
-            load_scale_rows(w2_scale, w2_scales[0], q)
-        w2_code = early.tile([P, 2 * H], U8, offset=12288, align_bytes=64)
+        load_scale_rows(w2_scale, w2_scales)
+        w2_code = early.tile([P, 2 * H], U8, offset=3 * PAGE_BYTES, align_bytes=64)
         nc.sync.dma_start(w2_code[:].bitcast(I32), w2_words[0].bitcast(I32))
         t2_code = early.tile([P, T2], I32, offset=0, align_bytes=64)
-        nc.sync.dma_start(t2_code[:], tab2_words[0].rearrange("p n t -> p (n t)").bitcast(I32))
-        for q in range(4):
-            load_scale_rows(t2_scale, tab2_scales[0], q)
-        wgs_sb = keep.tile([P, PACK, PL], F32)
-        for q in range(4):
-            nc.sync.dma_start(wgs_sb[32 * q : 32 * q + 32, :, :], wgs.rearrange("(p t) j -> p t j", t=PACK))
+        nc.sync.dma_start(t2_code[:], tab2_words[0].rearrange("p n i -> p (n i)").bitcast(I32))
+        load_scale_rows(t2_scale, tab2_scales)
+        wgs_sb = keep.tile([P, PACK, SOAKED], F32)
+        for u in range(4):
+            nc.sync.dma_start(wgs_sb[32 * u : 32 * u + 32, :, :], wgs.rearrange("(p t) j -> p t j", t=PACK))
 
-        w1_raw = {}
-        for g in range(2):
-            for a in range(3):
-                w1_raw[a, g] = raw.tile([P, PACK, HALF], F32, name="raw")
-                nc.sync.dma_start(
-                    w1_raw[a, g][:],
-                    w1[a * KP : (a + 1) * KP, g * KP : (g + 1) * KP].rearrange("(p i) c -> p i c", i=PACK),
-                )
-        w4_raw = {}
-        for g in range(2):
-            w4_raw[g] = raw.tile([P, PACK, N], F32, name="raw")
-            nc.sync.dma_start(w4_raw[g][:], w4[g * KP : (g + 1) * KP, :].rearrange("(p i) c -> p i c", i=PACK))
-        idx = lists.tile([P, S // 16], U16)
+        w1_raw = {
+            (a, g): load_rows(w1[a * PASS : (a + 1) * PASS, g * PASS : (g + 1) * PASS])
+            for g in range(2)
+            for a in range(3)
+        }
+        w4_raw = [load_rows(w4[g * PASS : (g + 1) * PASS, :]) for g in range(2)]
+        idx = lists.tile([P, S // PER_COL], U16)
         nc.sync.dma_start(idx[:], offs)
         gain_sb = keep.tile([P, 2, PACK], F32)
         nc.sync.dma_start(gain_sb[:], gain.rearrange("(g p t) -> p g t", g=2, t=PACK))
-        for q in range(4):
-            nc.sync.dma_start(t1_scale[32 * q : 32 * q + 12, :].bitcast(I32), tab_scales[:, 4 * q : 4 * q + 4, :].bitcast(I32))
+        load_scale_rows(t1_scale, tab_scales)
         t1_code = []
         for a in range(3):
             t1_code.append(big.tile([P, T], I32, name="big", align_bytes=64))
-            nc.sync.dma_start(t1_code[a][:], tab_words[a].rearrange("p n t -> p (n t)").bitcast(I32))
-        blank_late = keep.tile([P, 2, 1], F32)
-        with nc.allow_non_contiguous_dma(reason="one value a row"):
-            nc.sync.dma_start(blank_late[:], blank_rows[:, :, PACK - 1 :])
-        lot_rows = lot.rearrange("(p t) j -> p t j", t=PACK)
-        y_sb = []
-        for h in range(2):
-            y_sb.append(raw.tile([P, PACK, HALF], F32, name="raw"))
-            nc.sync.dma_start(y_sb[h][:], lot_rows[:, :, h * HALF : (h + 1) * HALF])
+            nc.sync.dma_start(t1_code[a][:], tab_words[a].rearrange("p n i -> p (n i)").bitcast(I32))
+        blank_g1_late = keep.tile([P, PACK - EARLY_T], F32)
+        nc.sync.dma_start(blank_g1_late[:], blank_rows[:, 1, EARLY_T:])
+        y_sb = [load_rows(lot[:, h * BANK : (h + 1) * BANK]) for h in range(2)]
 
         w2_dealt = keep.tile([P, 2, PACK, P], U16, align_bytes=64)
         w2_scale_dealt = keep.tile([P, 2, PACK, P], U8, align_bytes=64)
-        w2_view = w2_code[:].bitcast(U16).rearrange("p (g m t) -> p g t m", g=2, t=PACK)
-        nc.vector.tensor_copy(w2_dealt[:], w2_view)
+        nc.vector.tensor_copy(w2_dealt[:], w2_code[:].bitcast(U16).rearrange("p (g m t) -> p g t m", g=2, t=PACK))
         nc.vector.tensor_copy(w2_scale_dealt[:], w2_scale[:].rearrange("p (g m t) -> p g t m", g=2, t=PACK))
-        v2_code = keep.tile([P, PL], U32, align_bytes=64)
-        v2_scale = keep.tile([P, PL], U8, align_bytes=64)
-        list_halves = [(0, PL // 2), (PL // 2, PL)]
+        v2_code = keep.tile([P, SOAKED], U32, align_bytes=64)
+        v2_scale = keep.tile([P, SOAKED], U8, align_bytes=64)
+        list_halves = [(0, SOAKED // 2), (SOAKED // 2, SOAKED)]
         for j0, j1 in list_halves:
-            nc.vector.tensor_copy(v2_code[:, j0:j1], t2_code[:].bitcast(U32).indirect(idx2[:, j0 // 16 : j1 // 16]))
-            nc.vector.tensor_copy(v2_scale[:, j0:j1], t2_scale[:].indirect(idx2[:, j0 // 16 : j1 // 16]))
-        for n, (g, t) in enumerate(order[4:]):
-            pages[g, t] = early.tile([P, S], F32, name=f"page{g}{t}", offset=4096 * n, align_bytes=64)
-            nc.gpsimd.memset(pages[g, t][:].bitcast(I32), 0)
+            nc.vector.tensor_copy(v2_code[:, j0:j1], t2_code[:].bitcast(U32).indirect(entries(idx2, j0, j1)))
+            nc.vector.tensor_copy(v2_scale[:, j0:j1], t2_scale[:].indirect(entries(idx2, j0, j1)))
+        for t in range(PACK):
+            pages[1, t] = early.tile([P, S], F32, name=f"page1{t}", offset=t * PAGE_BYTES, align_bytes=64)
+            nc.gpsimd.memset(pages[1, t][:].bitcast(I32), 0)
 
         v_scale = keep.tile([P, S], U8, align_bytes=64)
         nc.vector.tensor_copy(v_scale[:], t1_scale[:].indirect(idx[:]))
         v_code = [keep.tile([P, S], U32, name=f"v_code{a}", align_bytes=64) for a in range(3)]
-        for a in range(2):
-            nc.vector.tensor_copy(v_code[a][:], t1_code[a][:].bitcast(U32).indirect(idx[:]))
-        for h in range(2):
-            nc.vector.tensor_copy(
-                v_code[2][:, h * HALF : (h + 1) * HALF],
-                t1_code[2][:].bitcast(U32).indirect(idx[:, h * HALF // 16 : (h + 1) * HALF // 16]),
-            )
+        for a in range(3):
+            for j0, j1 in [(0, BANK), (BANK, S)] if a == 2 else [(0, S)]:
+                nc.vector.tensor_copy(v_code[a][:, j0:j1], t1_code[a][:].bitcast(U32).indirect(entries(idx, j0, j1)))
 
-        for g, t in order:
-            if g == 0:
-                b_pair = rows.tile([P, 2, PL], F32, name="rows")
-            bias = blank_early[:, g, t : t + 1] if t < PACK - 1 else blank_late[:, g, :]
-            for j0, j1 in list_halves if (g, t) == order[0] else [(0, PL)]:
-                acc_b = psum.tile([P, PL], F32, name="acc")
-                nc.tensor.matmul_mx(
-                    out=acc_b[:, j0:j1],
-                    lhsT=w2_dealt[:, g, t, :].bitcast(FP4X4),
-                    lhsT_scale=w2_scale_dealt[:, g, t, :],
-                    rhs=v2_code[:, j0:j1].bitcast(FP8X4),
-                    rhs_scale=v2_scale[:, j0:j1],
-                    start=True,
-                    stop=True,
-                )
-                nc.scalar.activation(b_pair[:, g, j0:j1], acc_b[:, j0:j1], ACT.Identity, bias=bias)
-                nc.vector.tensor_tensor(
-                    pages[g, t][:].indirect(seats[:, j0 // 16 : j1 // 16]),
-                    b_pair[:, g, j0:j1],
-                    wgs_sb[:, t, j0:j1],
-                    ALU.mult,
-                )
+        for g in range(2):
+            for t in range(PACK):
+                if t % 2 == 0:
+                    b_pair = rows.tile([P, 2, SOAKED], F32, name="rows")
+                if g == 0:
+                    bias = blank_g0[:, t : t + 1]
+                elif t < EARLY_T:
+                    bias = blank_g1_early[:, t : t + 1]
+                else:
+                    bias = blank_g1_late[:, t - EARLY_T : t - EARLY_T + 1]
+                for j0, j1 in list_halves if (g, t) == (0, 0) else [(0, SOAKED)]:
+                    acc_b = bank()
+                    nc.tensor.matmul_mx(
+                        out=acc_b[:, j0:j1],
+                        lhsT=w2_dealt[:, g, t, :].bitcast(FP4X4),
+                        lhsT_scale=w2_scale_dealt[:, g, t, :],
+                        rhs=v2_code[:, j0:j1].bitcast(FP8X4),
+                        rhs_scale=v2_scale[:, j0:j1],
+                        start=True,
+                        stop=True,
+                    )
+                    nc.scalar.activation(b_pair[:, t % 2, j0:j1], acc_b[:, j0:j1], ACT.Identity, bias=bias)
+                    nc.vector.tensor_tensor(
+                        pages[g, t][:].indirect(entries(seats, j0, j1)),
+                        b_pair[:, t % 2, j0:j1],
+                        wgs_sb[:, t, j0:j1],
+                        ALU.mult,
+                    )
 
-        def quantize_weight(raw_rows, dealt, name):
-            woven = stage.tile([P, HALF, PACK], BF16, name="woven", align_bytes=64)
+        def quantize_weight(piece, dealt, name):
+            woven = woven_tile()
             if dealt:
                 nc.scalar.copy(
                     out=woven[:].rearrange("p (t m) i -> p m i t", t=PACK),
-                    in_=raw_rows[:].rearrange("p i (m t) -> p m i t", t=PACK),
+                    in_=piece[:].rearrange("p i (m t) -> p m i t", t=PACK),
                 )
             else:
-                weave(woven, raw_rows, HALF)
-            code = keep.tile([P, HALF], U32, name=name + "_code", align_bytes=64)
-            scale = keep.tile([P, HALF], U8, name=name + "_scale", align_bytes=64)
-            quantize(code[:], scale[:], woven[:].rearrange("p c i -> p (c i)"))
-            return code, scale
+                weave(woven, piece, BANK)
+            return quantize(woven, name)
 
-        w1_code, w1_scale, w4_code, w4_scale = {}, {}, {}, {}
-        for g in range(2):
-            for a in range(3):
-                w1_code[a, g], w1_scale[a, g] = quantize_weight(w1_raw[a, g], True, f"w1_{a}{g}")
-        for g in range(2):
-            w4_code[g], w4_scale[g] = quantize_weight(w4_raw[g], True, f"w4_{g}")
+        w1_mx = {(a, g): quantize_weight(w1_raw[a, g], g == 1, f"w1_{a}{g}") for g in range(2) for a in range(3)}
+        w4_mx = [quantize_weight(w4_raw[g], True, f"w4_{g}") for g in range(2)]
 
-        z_code, z_scale = {}, {}
+        z_mx = {}
 
-        def make_z(g, h):
-            cols = slice(h * HALF, (h + 1) * HALF)
-            rest = big.tile([P, PACK, HALF], F32, name="big", align_bytes=64)
-            z_rows = rows.tile([P, PACK, HALF], BF16, name="rows")
-            for t in range(PACK):
-                acc_f = psum.tile([P, HALF], F32, name="acc")
+        def finish_z(g, h, z_rows):
+            woven = woven_tile()
+            weave(woven, z_rows, BANK)
+            z_mx[g, h] = quantize(woven, f"z_{g}{h}")
+
+        def gain_and_place(z_rows, u, g, t, h):
+            nc.vector.scalar_tensor_tensor(
+                out=z_rows[:, t, :],
+                in0=u,
+                scalar=gain_sb[:, g, t : t + 1],
+                in1=pages[g, t][:, h * BANK : (h + 1) * BANK],
+                op0=ALU.mult,
+                op1=ALU.add,
+            )
+
+        def transposed_terms(g, h):
+            terms = big.tile([P, 4, 2, PASS], F32, name="big", align_bytes=64)
+            for c in range(4):
+                cols = slice(h * BANK + c * P, h * BANK + (c + 1) * P)
+                acc_f = bank()
                 for a in range(3):
                     nc.tensor.matmul_mx(
                         out=acc_f[:],
-                        lhsT=w1_code[a, g][:, t * P : (t + 1) * P].bitcast(FP8X4),
-                        lhsT_scale=w1_scale[a, g][:, t * P : (t + 1) * P],
+                        lhsT=v_code[a][:, cols].bitcast(FP8X4),
+                        lhsT_scale=v_scale[4 * a : P, cols],
+                        rhs=w1_mx[a, g][0][:].bitcast(FP8X4),
+                        rhs_scale=w1_mx[a, g][1][:],
+                        start=(a == 0),
+                        stop=(a == 2),
+                    )
+                by_slice = acc_f[:].rearrange("j (p t) -> j t p", t=PACK)
+                nc.scalar.activation(terms[:, c, 0, :].rearrange("j (t p) -> j t p", t=PACK), by_slice, ACT.Tanh)
+                nc.scalar.copy(terms[:, c, 1, :].rearrange("j (t p) -> j t p", t=PACK), by_slice)
+            return terms
+
+        def z_from_terms(g, h, terms):
+            z_rows = rows.tile([P, PACK, BANK], BF16, name="rows")
+            for t in range(PACK):
+                acc_u = bank()
+                for c in range(4):
+                    for term in range(2):
+                        nc.tensor.matmul(
+                            acc_u[:, c * P : (c + 1) * P],
+                            terms[:, c, term, t * P : (t + 1) * P],
+                            ident[:],
+                            start=(term == 0),
+                            stop=(term == 1),
+                            is_transpose=True,
+                        )
+                gain_and_place(z_rows, acc_u[:], g, t, h)
+            finish_z(g, h, z_rows)
+
+        def z_direct(g, h):
+            cols = slice(h * BANK, (h + 1) * BANK)
+            u = big.tile([P, PACK, BANK], F32, name="big", align_bytes=64)
+            z_rows = rows.tile([P, PACK, BANK], BF16, name="rows")
+            for t in range(PACK):
+                acc_f = bank()
+                for a in range(3):
+                    nc.tensor.matmul_mx(
+                        out=acc_f[:],
+                        lhsT=w1_mx[a, g][0][:, t * P : (t + 1) * P].bitcast(FP8X4),
+                        lhsT_scale=w1_mx[a, g][1][:, t * P : (t + 1) * P],
                         rhs=v_code[a][:, cols].bitcast(FP8X4),
                         rhs_scale=v_scale[4 * a : P, cols],
                         start=(a == 0),
                         stop=(a == 2),
                     )
-                nc.scalar.activation(rest[:, t, :], acc_f[:], ACT.Tanh)
-                nc.scalar.activation(rest[:, t, :], rest[:, t, :], ACT.Copy, scale=gain_sb[:, g, t : t + 1])
-                nc.gpsimd.tensor_tensor(rest[:, t, :], rest[:, t, :], pages[g, t][:, cols], ALU.add)
-                nc.vector.scalar_tensor_tensor(
-                    out=z_rows[:, t, :],
-                    in0=acc_f[:],
-                    scalar=gain_sb[:, g, t : t + 1],
-                    in1=rest[:, t, :],
-                    op0=ALU.mult,
-                    op1=ALU.add,
-                )
+                nc.scalar.activation(u[:, t, :], acc_f[:], ACT.Tanh)
+                nc.vector.tensor_tensor(u[:, t, :], acc_f[:], u[:, t, :], ALU.add)
+                if t > 0:
+                    gain_and_place(z_rows, u[:, t - 1, :], g, t - 1, h)
+            gain_and_place(z_rows, u[:, PACK - 1, :], g, PACK - 1, h)
             finish_z(g, h, z_rows)
 
-        def finish_z(g, h, z_rows):
-            woven = stage.tile([P, HALF, PACK], BF16, name="woven", align_bytes=64)
-            weave(woven, z_rows, Z_ON_SCALAR[g, h])
-            z_code[g, h] = keep.tile([P, HALF], U32, name=f"z_code{g}{h}", align_bytes=64)
-            z_scale[g, h] = keep.tile([P, HALF], U8, name=f"z_scale{g}{h}", align_bytes=64)
-            quantize(z_code[g, h][:], z_scale[g, h][:], woven[:].rearrange("p c i -> p (c i)"))
-
         out_rows = out_0.rearrange("(p t) j -> p t j", t=PACK)
-        out_words = out_1[0].rearrange("p m t -> p (m t)").bitcast(I32)
+        out_words = out_1[0].rearrange("p j t -> p (j t)").bitcast(I32)
 
-        def last_stage(h):
-            cols = slice(h * HALF, (h + 1) * HALF)
+        def last_stage(h, on_scalar):
+            cols = slice(h * BANK, (h + 1) * BANK)
+            acc_y = [bank() for t in range(PACK)]
             for t in range(PACK):
-                acc_y = psum.tile([P, HALF], F32, name="acc")
                 for g in range(2):
                     nc.tensor.matmul_mx(
-                        out=acc_y[:],
-                        lhsT=w4_code[g][:, t * P : (t + 1) * P].bitcast(FP8X4),
-                        lhsT_scale=w4_scale[g][:, t * P : (t + 1) * P],
-                        rhs=z_code[g, h][:].bitcast(FP8X4),
-                        rhs_scale=z_scale[g, h][:],
+                        out=acc_y[t][:],
+                        lhsT=w4_mx[g][0][:, t * P : (t + 1) * P].bitcast(FP8X4),
+                        lhsT_scale=w4_mx[g][1][:, t * P : (t + 1) * P],
+                        rhs=z_mx[g, h][0][:].bitcast(FP8X4),
+                        rhs_scale=z_mx[g, h][1][:],
                         start=(g == 0),
                         stop=(g == 1),
                     )
-                nc.vector.tensor_tensor(y_sb[h][:, t, :], acc_y[:], y_sb[h][:, t, :], ALU.add)
+            for t in range(PACK):
+                nc.vector.tensor_tensor(y_sb[h][:, t, :], acc_y[t][:], y_sb[h][:, t, :], ALU.add)
                 nc.sync.dma_start(out_rows[:, t, cols], y_sb[h][:, t, :])
-            woven = stage.tile([P, HALF, PACK], BF16, name="woven", align_bytes=64)
-            weave(woven, y_sb[h], Y_ON_SCALAR[h])
-            y_code = keep.tile([P, HALF], U32, name=f"y_code{h}", align_bytes=64)
-            y_scale = keep.tile([P, HALF], U8, name=f"y_scale{h}", align_bytes=64)
-            quantize(y_code[:], y_scale[:], woven[:].rearrange("p c i -> p (c i)"))
+            woven = woven_tile()
+            weave(woven, y_sb[h], on_scalar)
+            y_code, y_scale = quantize(woven, f"y_{h}")
             nc.sync.dma_start(out_words[:, cols], y_code[:].bitcast(I32))
-            for q in range(4):
-                nc.sync.dma_start(
-                    out_2[0, 4 * q : 4 * q + 4, cols].bitcast(I32), y_scale[32 * q : 32 * q + 4, :].bitcast(I32)
+            for u in range(4):
+                (nc.sync if u % 2 else nc.scalar).dma_start(
+                    out_2[0, 4 * u : 4 * u + 4, cols].bitcast(I32), y_scale[32 * u : 32 * u + 4, :].bitcast(I32)
                 )
 
-        make_z(0, 0)
-        make_z(1, 0)
-        make_z(0, 1)
-        last_stage(0)
-        make_z(1, 1)
-        last_stage(1)
+        terms = [transposed_terms(0, h) for h in range(2)]
+        for h in range(2):
+            z_from_terms(0, h, terms[h])
+        for h in range(2):
+            z_direct(1, h)
+        last_stage(0, BANK)
+        last_stage(1, LAST_WEAVE_ON_SCALAR)

from contextlib import ExitStack

import concourse.mybir as mybir
from concourse.masks import make_identity

K, K2, T, T2, S, SOAKED, H, N = 1536, 512, 4096, 2048, 1024, 512, 1024, 512
FLOPS = 2 * (K * H * S + K2 * H * SOAKED + H * N * S)

F32 = mybir.dt.float32
BF16 = mybir.dt.bfloat16
I32 = mybir.dt.int32
U32 = mybir.dt.uint32
U16 = mybir.dt.uint16
U8 = mybir.dt.uint8
FP8X4 = mybir.dt.float8_e4m3fn_x4
FP4X4 = mybir.dt.float4_e2m1fn_x4
ACT = mybir.ActivationFunctionType
ALU = mybir.AluOpType

P = 128
PACK = 4
PASS = P * PACK
BANK = 512
PER_COL = 16
PAGE_BYTES = 4 * S
EARLY_T = 2
LAST_WEAVE_ON_SCALAR = 176


def tile_list_cork_taint_features_kernel(
    tc, tab_words, tab_scales, tab2_words, tab2_scales, offs, offs2, pos1, w1, gain,
    w2_words, w2_scales, blank, wgs, w4, lot, out_0, out_1, out_2,
):
    nc = tc.nc

    def entries(offsets, j0, j1):
        return offsets[:, j0 // PER_COL : j1 // PER_COL]

    def weave(woven, rows, on_scalar):
        shares = ((nc.scalar.copy, 0, on_scalar), (nc.vector.tensor_copy, on_scalar, BANK))
        for engine_copy, j0, j1 in shares:
            if j1 > j0:
                engine_copy(
                    out=woven[:, j0:j1, :].rearrange("p (c i) t -> p c t i", i=4),
                    in_=rows[:, :, j0:j1].rearrange("p t (c i) -> p c t i", i=4),
                )

    with ExitStack() as ctx:
        lists = ctx.enter_context(tc.tile_pool(name="lists", bufs=1))
        keep = ctx.enter_context(tc.tile_pool(name="keep", bufs=1))
        early = ctx.enter_context(tc.tile_pool(name="early", bufs=1))
        big = ctx.enter_context(tc.tile_pool(name="big", bufs=3))
        raw = ctx.enter_context(tc.tile_pool(name="raw", bufs=5))
        rows = ctx.enter_context(tc.tile_pool(name="rows", bufs=4))
        stage = ctx.enter_context(tc.tile_pool(name="stage", bufs=8))
        psum = ctx.enter_context(tc.psum_pool(name="psum", bufs=8))

        def bank():
            return psum.tile([P, BANK], F32, name="bank")

        def woven_tile():
            return stage.tile([P, BANK, PACK], BF16, name="woven", align_bytes=64)

        def quantize(woven, name):
            code = keep.tile([P, BANK], U32, name=name + "_code", align_bytes=64)
            scale = keep.tile([P, BANK], U8, name=name + "_scale", align_bytes=64)
            nc.vector.quantize_mx(
                out=code[:].bitcast(FP8X4), scales=scale[:], in_=woven[:].rearrange("p j t -> p (j t)")
            )
            return code, scale

        t2_scale = early.tile([P, T2], U8, offset=2 * PAGE_BYTES, align_bytes=64)
        w2_scale = early.tile([P, H], U8, offset=3 * PAGE_BYTES + 2 * H, align_bytes=64)
        t1_scale = keep.tile([P, T], U8, align_bytes=64)
        nc.gpsimd.memset(w2_scale[:].bitcast(I32), 0)
        blank_rows = blank.rearrange("(g p t) -> p g t", g=2, t=PACK)
        blank_g0 = keep.tile([P, PACK], F32)
        nc.gpsimd.dma_start(blank_g0[:], blank_rows[:, 0, :])
        blank_g1_early = keep.tile([P, EARLY_T], F32)
        nc.gpsimd.dma_start(blank_g1_early[:], blank_rows[:, 1, :EARLY_T])
        nc.vector.memset(t2_scale[:].bitcast(I32), 0)
        pages = {}
        for t in range(PACK):
            pages[0, t] = keep.tile([P, S], F32, name=f"page0{t}")
            (nc.vector if t < 2 else nc.gpsimd).memset(pages[0, t][:].bitcast(I32), 0)
        nc.gpsimd.memset(t1_scale[:].bitcast(I32), 0)
        ident = keep.tile([P, P], F32)
        make_identity(nc, ident[:])

        def load_scale_rows(plane, scale_rows):
            passes = scale_rows.shape[0]
            for u in range(4):
                nc.sync.dma_start(
                    plane[32 * u : 32 * u + 4 * passes, :].bitcast(I32),
                    scale_rows[:, 4 * u : 4 * u + 4, :].bitcast(I32),
                )

        def load_rows(source):
            piece = raw.tile([P, PACK, BANK], F32, name="raw")
            nc.sync.dma_start(piece[:], source.rearrange("(p i) c -> p i c", i=PACK))
            return piece

        idx2 = lists.tile([P, SOAKED // PER_COL], U16)
        nc.sync.dma_start(idx2[:], offs2)
        seats = lists.tile([P, SOAKED // PER_COL], U16)
        nc.sync.dma_start(seats[:], pos1)
        load_scale_rows(w2_scale, w2_scales)
        w2_code = early.tile([P, 2 * H], U8, offset=3 * PAGE_BYTES, align_bytes=64)
        nc.sync.dma_start(w2_code[:].bitcast(I32), w2_words[0].bitcast(I32))
        t2_code = early.tile([P, T2], I32, offset=0, align_bytes=64)
        nc.sync.dma_start(t2_code[:], tab2_words[0].rearrange("p n i -> p (n i)").bitcast(I32))
        load_scale_rows(t2_scale, tab2_scales)
        wgs_sb = keep.tile([P, PACK, SOAKED], F32)
        for u in range(4):
            nc.sync.dma_start(wgs_sb[32 * u : 32 * u + 32, :, :], wgs.rearrange("(p t) j -> p t j", t=PACK))

        w1_raw = {
            (a, g): load_rows(w1[a * PASS : (a + 1) * PASS, g * PASS : (g + 1) * PASS])
            for g in range(2)
            for a in range(3)
        }
        w4_raw = [load_rows(w4[g * PASS : (g + 1) * PASS, :]) for g in range(2)]
        idx = lists.tile([P, S // PER_COL], U16)
        nc.sync.dma_start(idx[:], offs)
        gain_sb = keep.tile([P, 2, PACK], F32)
        nc.sync.dma_start(gain_sb[:], gain.rearrange("(g p t) -> p g t", g=2, t=PACK))
        load_scale_rows(t1_scale, tab_scales)
        t1_code = []
        for a in range(3):
            t1_code.append(big.tile([P, T], I32, name="big", align_bytes=64))
            nc.sync.dma_start(t1_code[a][:], tab_words[a].rearrange("p n i -> p (n i)").bitcast(I32))
        blank_g1_late = keep.tile([P, PACK - EARLY_T], F32)
        nc.sync.dma_start(blank_g1_late[:], blank_rows[:, 1, EARLY_T:])
        y_sb = [load_rows(lot[:, h * BANK : (h + 1) * BANK]) for h in range(2)]

        w2_dealt = keep.tile([P, 2, PACK, P], U16, align_bytes=64)
        w2_scale_dealt = keep.tile([P, 2, PACK, P], U8, align_bytes=64)
        nc.vector.tensor_copy(w2_dealt[:], w2_code[:].bitcast(U16).rearrange("p (g m t) -> p g t m", g=2, t=PACK))
        nc.vector.tensor_copy(w2_scale_dealt[:], w2_scale[:].rearrange("p (g m t) -> p g t m", g=2, t=PACK))
        v2_code = keep.tile([P, SOAKED], U32, align_bytes=64)
        v2_scale = keep.tile([P, SOAKED], U8, align_bytes=64)
        list_halves = [(0, SOAKED // 2), (SOAKED // 2, SOAKED)]
        for j0, j1 in list_halves:
            nc.vector.tensor_copy(v2_code[:, j0:j1], t2_code[:].bitcast(U32).indirect(entries(idx2, j0, j1)))
            nc.vector.tensor_copy(v2_scale[:, j0:j1], t2_scale[:].indirect(entries(idx2, j0, j1)))
        for t in range(PACK):
            pages[1, t] = early.tile([P, S], F32, name=f"page1{t}", offset=t * PAGE_BYTES, align_bytes=64)
            nc.gpsimd.memset(pages[1, t][:].bitcast(I32), 0)

        v_scale = keep.tile([P, S], U8, align_bytes=64)
        nc.vector.tensor_copy(v_scale[:], t1_scale[:].indirect(idx[:]))
        v_code = [keep.tile([P, S], U32, name=f"v_code{a}", align_bytes=64) for a in range(3)]
        for a in range(3):
            for j0, j1 in [(0, BANK), (BANK, S)] if a == 2 else [(0, S)]:
                nc.vector.tensor_copy(v_code[a][:, j0:j1], t1_code[a][:].bitcast(U32).indirect(entries(idx, j0, j1)))

        for g in range(2):
            for t in range(PACK):
                if t % 2 == 0:
                    b_pair = rows.tile([P, 2, SOAKED], F32, name="rows")
                if g == 0:
                    bias = blank_g0[:, t : t + 1]
                elif t < EARLY_T:
                    bias = blank_g1_early[:, t : t + 1]
                else:
                    bias = blank_g1_late[:, t - EARLY_T : t - EARLY_T + 1]
                for j0, j1 in list_halves if (g, t) == (0, 0) else [(0, SOAKED)]:
                    acc_b = bank()
                    nc.tensor.matmul_mx(
                        out=acc_b[:, j0:j1],
                        lhsT=w2_dealt[:, g, t, :].bitcast(FP4X4),
                        lhsT_scale=w2_scale_dealt[:, g, t, :],
                        rhs=v2_code[:, j0:j1].bitcast(FP8X4),
                        rhs_scale=v2_scale[:, j0:j1],
                        start=True,
                        stop=True,
                    )
                    nc.scalar.activation(b_pair[:, t % 2, j0:j1], acc_b[:, j0:j1], ACT.Identity, bias=bias)
                    nc.vector.tensor_tensor(
                        pages[g, t][:].indirect(entries(seats, j0, j1)),
                        b_pair[:, t % 2, j0:j1],
                        wgs_sb[:, t, j0:j1],
                        ALU.mult,
                    )

        def quantize_weight(piece, dealt, name):
            woven = woven_tile()
            if dealt:
                nc.scalar.copy(
                    out=woven[:].rearrange("p (t m) i -> p m i t", t=PACK),
                    in_=piece[:].rearrange("p i (m t) -> p m i t", t=PACK),
                )
            else:
                weave(woven, piece, BANK)
            return quantize(woven, name)

        w1_mx = {(a, g): quantize_weight(w1_raw[a, g], g == 1, f"w1_{a}{g}") for g in range(2) for a in range(3)}
        w4_mx = [quantize_weight(w4_raw[g], True, f"w4_{g}") for g in range(2)]

        z_mx = {}

        def finish_z(g, h, z_rows):
            woven = woven_tile()
            weave(woven, z_rows, BANK)
            z_mx[g, h] = quantize(woven, f"z_{g}{h}")

        def gain_and_place(z_rows, u, g, t, h):
            nc.vector.scalar_tensor_tensor(
                out=z_rows[:, t, :],
                in0=u,
                scalar=gain_sb[:, g, t : t + 1],
                in1=pages[g, t][:, h * BANK : (h + 1) * BANK],
                op0=ALU.mult,
                op1=ALU.add,
            )

        def transposed_terms(g, h):
            terms = big.tile([P, 4, 2, PASS], F32, name="big", align_bytes=64)
            for c in range(4):
                cols = slice(h * BANK + c * P, h * BANK + (c + 1) * P)
                acc_f = bank()
                for a in range(3):
                    nc.tensor.matmul_mx(
                        out=acc_f[:],
                        lhsT=v_code[a][:, cols].bitcast(FP8X4),
                        lhsT_scale=v_scale[4 * a : P, cols],
                        rhs=w1_mx[a, g][0][:].bitcast(FP8X4),
                        rhs_scale=w1_mx[a, g][1][:],
                        start=(a == 0),
                        stop=(a == 2),
                    )
                by_slice = acc_f[:].rearrange("j (p t) -> j t p", t=PACK)
                nc.scalar.activation(terms[:, c, 0, :].rearrange("j (t p) -> j t p", t=PACK), by_slice, ACT.Tanh)
                nc.scalar.copy(terms[:, c, 1, :].rearrange("j (t p) -> j t p", t=PACK), by_slice)
            return terms

        def z_from_terms(g, h, terms):
            z_rows = rows.tile([P, PACK, BANK], BF16, name="rows")
            for t in range(PACK):
                acc_u = bank()
                for c in range(4):
                    for term in range(2):
                        nc.tensor.matmul(
                            acc_u[:, c * P : (c + 1) * P],
                            terms[:, c, term, t * P : (t + 1) * P],
                            ident[:],
                            start=(term == 0),
                            stop=(term == 1),
                            is_transpose=True,
                        )
                gain_and_place(z_rows, acc_u[:], g, t, h)
            finish_z(g, h, z_rows)

        def z_direct(g, h):
            cols = slice(h * BANK, (h + 1) * BANK)
            u = big.tile([P, PACK, BANK], F32, name="big", align_bytes=64)
            z_rows = rows.tile([P, PACK, BANK], BF16, name="rows")
            for t in range(PACK):
                acc_f = bank()
                for a in range(3):
                    nc.tensor.matmul_mx(
                        out=acc_f[:],
                        lhsT=w1_mx[a, g][0][:, t * P : (t + 1) * P].bitcast(FP8X4),
                        lhsT_scale=w1_mx[a, g][1][:, t * P : (t + 1) * P],
                        rhs=v_code[a][:, cols].bitcast(FP8X4),
                        rhs_scale=v_scale[4 * a : P, cols],
                        start=(a == 0),
                        stop=(a == 2),
                    )
                nc.scalar.activation(u[:, t, :], acc_f[:], ACT.Tanh)
                nc.vector.tensor_tensor(u[:, t, :], acc_f[:], u[:, t, :], ALU.add)
                if t > 0:
                    gain_and_place(z_rows, u[:, t - 1, :], g, t - 1, h)
            gain_and_place(z_rows, u[:, PACK - 1, :], g, PACK - 1, h)
            finish_z(g, h, z_rows)

        out_rows = out_0.rearrange("(p t) j -> p t j", t=PACK)
        out_words = out_1[0].rearrange("p j t -> p (j t)").bitcast(I32)

        def last_stage(h, on_scalar):
            cols = slice(h * BANK, (h + 1) * BANK)
            acc_y = [bank() for t in range(PACK)]
            for t in range(PACK):
                for g in range(2):
                    nc.tensor.matmul_mx(
                        out=acc_y[t][:],
                        lhsT=w4_mx[g][0][:, t * P : (t + 1) * P].bitcast(FP8X4),
                        lhsT_scale=w4_mx[g][1][:, t * P : (t + 1) * P],
                        rhs=z_mx[g, h][0][:].bitcast(FP8X4),
                        rhs_scale=z_mx[g, h][1][:],
                        start=(g == 0),
                        stop=(g == 1),
                    )
            for t in range(PACK):
                nc.vector.tensor_tensor(y_sb[h][:, t, :], acc_y[t][:], y_sb[h][:, t, :], ALU.add)
                nc.sync.dma_start(out_rows[:, t, cols], y_sb[h][:, t, :])
            woven = woven_tile()
            weave(woven, y_sb[h], on_scalar)
            y_code, y_scale = quantize(woven, f"y_{h}")
            nc.sync.dma_start(out_words[:, cols], y_code[:].bitcast(I32))
            for u in range(4):
                (nc.sync if u % 2 else nc.scalar).dma_start(
                    out_2[0, 4 * u : 4 * u + 4, cols].bitcast(I32), y_scale[32 * u : 32 * u + 4, :].bitcast(I32)
                )

        terms = [transposed_terms(0, h) for h in range(2)]
        for h in range(2):
            z_from_terms(0, h, terms[h])
        for h in range(2):
            z_direct(1, h)
        last_stage(0, BANK)
        last_stage(1, LAST_WEAVE_ON_SCALAR)
